import numpy as np
import ml_dtypes


def mxq(x, axis, fmt="e4m3"):
    dtype, down = {"e4m3": (ml_dtypes.float8_e4m3fn, 7), "e5m2": (ml_dtypes.float8_e5m2, 14)}[fmt]
    v = np.moveaxis(np.asarray(x, np.float32).astype(ml_dtypes.bfloat16).astype(np.float64), axis, -1)
    blocks = v.reshape(v.shape[:-1] + (-1, 32))
    amax = np.abs(blocks).max(-1, keepdims=True)
    byte = np.maximum(np.where(amax > 0, np.frexp(amax)[1] - 1 + 127, 0) - down, 1)
    scale = np.exp2(byte - 127.0)
    codes = (blocks / scale).astype(np.float32).astype(dtype).astype(np.float64)
    return np.moveaxis((codes * scale).reshape(v.shape), -1, axis)


WIDE = False


def mx_kscale(k):
    if not WIDE:
        return np.ones(k)
    levels = np.array([30, -30])
    if k % 512:
        return np.exp2(np.random.permutation(np.resize(levels, k // 32))).repeat(32)
    a = np.empty((k // 512, 16))
    for p in range(k // 512):
        a[p, :8] = np.random.permutation(np.resize(levels, 8))
        for g in range(8):
            far = levels[np.abs(levels - a[p, g]) >= 10]
            a[p, g + 8] = far[np.random.randint(len(far))]
    return np.exp2(a.ravel()).repeat(32)


def f64(x):
    return np.asarray(x).astype(np.float64)


E2M1 = np.array([0.0, 0.5, 1.0, 1.5, 2.0, 3.0, 4.0, 6.0, -0.0, -0.5, -1.0, -1.5, -2.0, -3.0, -4.0, -6.0])


def pack_weight(w, fmt):
    k, n = w.shape
    w = f64(np.asarray(w, np.float32).astype(ml_dtypes.bfloat16)).reshape(k // 32, 32, n)
    amax = np.abs(w).max(1)
    if fmt == "e4m3":
        byte = np.frexp(amax)[1] - 1 + 127 - 7
    else:
        mant, ex = np.frexp(amax / 6.0)
        byte = np.where(mant > 0.5, ex, ex - 1) + 127
    byte = np.clip(np.where(amax > 0, byte, 1), 1, 254)
    scaled = (w * np.exp2(127.0 - byte)[:, None, :]).reshape(k, n).astype(np.float32)
    by_word = np.ascontiguousarray(scaled.reshape(k // 512, 128, 4, n).transpose(0, 1, 3, 2))
    if fmt == "e4m3":
        words = by_word.astype(ml_dtypes.float8_e4m3fn).view(np.uint8)
    else:
        c = by_word.astype(ml_dtypes.float4_e2m1fn).view(np.uint8) & 0xF
        words = (c[..., 0::2] | (c[..., 1::2] << 4)).reshape(k // 512, 128, 2 * n)
    return np.ascontiguousarray(words), np.ascontiguousarray(byte.astype(np.uint8).reshape(k // 512, 16, n))


def unpack_weight(words, scales, fmt):
    g, _, n = scales.shape
    words = np.ascontiguousarray(words).reshape(g, 128, n, -1)
    if fmt == "e4m3":
        vals = words.view(ml_dtypes.float8_e4m3fn).astype(np.float64)
    else:
        nib = np.empty((g, 128, n, 4), np.uint8)
        nib[..., 0::2] = words & 0xF
        nib[..., 1::2] = words >> 4
        vals = E2M1[nib]
    vals = vals * np.repeat(np.exp2(scales.astype(np.float64) - 127.0), 8, axis=1)[..., None]
    return vals.transpose(0, 1, 3, 2).reshape(g * 512, n)


O, T, D, H = 1024, 1536, 768, 1024


def setup_inputs():
    n = np.random.standard_normal
    s = mx_kscale(T)[:, None]
    m = np.exp(0.5 * n((T, 1)))
    x = n((T, D)) * s
    p_x4 = pack_weight(x[:O], "e2m1")
    return {
        "x4_words": p_x4[0],
        "x4_scales": p_x4[1],
        "x8": (x[O:]).astype(np.float32),
        "dy": (m * n((T, H)) / np.sqrt(T) / s).astype(np.float32),
        "mom": (n((768, 1024))).astype(np.float32),
    }


def reference(x4_words, x4_scales, x8, dy, mom):
    x4_ = unpack_weight(x4_words, x4_scales, "e2m1")
    x8_ = mxq(f64(x8), 0, "e4m3")
    dy_ = mxq(f64(dy), 0, "e5m2")
    y = x4_.T @ dy_[:O] + x8_.T @ dy_[O:]
    return 0.9 * f64(mom) + y

from contextlib import ExitStack

import concourse.mybir as mybir

T4, T8, D, H = 1024, 512, 768, 1024
FLOPS = 2 * (T4 + T8) * D * H

F32 = mybir.dt.float32
BF16 = mybir.dt.bfloat16
I32 = mybir.dt.int32
U32 = mybir.dt.uint32
U8 = mybir.dt.uint8
E4M3 = mybir.dt.float8_e4m3fn_x4
E5M2 = mybir.dt.float8_e5m2_x4
E2M1 = mybir.dt.float4_e2m1fn_x4
MULT = mybir.AluOpType.mult
ADD = mybir.AluOpType.add

P = 128
PACK = 4
NT = 512
DT = D // P
HT = H // NT
BANKS = 8
V_COLS = 640


def interleave(copy, grouped, raw, w0, w1):
    copy(
        out=grouped[:, w0:w1, :].rearrange("p (c i) j -> p c j i", i=4),
        in_=raw[:, :, w0:w1].rearrange("p j (c i) -> p c j i", i=4),
    )


def tile_mix_dwsav_ema_kernel(tc, x4_words, x4_scales, x8, dy, mom, out):
    nc = tc.nc
    with ExitStack() as ctx:
        keep = ctx.enter_context(tc.tile_pool(name="keep", bufs=1))
        psum = ctx.enter_context(tc.psum_pool(name="psum", bufs=1))
        ctx.enter_context(tc.manual_schedule())

        x4_codes = keep.tile([P, 2, 2 * D], U8, align_bytes=256)
        x4_plane = keep.tile([P, 2, D], U8, align_bytes=256)
        x8_raw = keep.tile([P, PACK, D], F32, align_bytes=256)
        x8_grouped = keep.tile([P, D, PACK], BF16, align_bytes=256)
        x8_codes = keep.tile([P, D], U32, align_bytes=256)
        x8_plane = keep.tile([P, D], U8, align_bytes=256)
        mom_sb = keep.tile([P, DT, H], F32, align_bytes=256)
        res = keep.tile([P, DT, H], F32, align_bytes=256)
        dy_raw, dy_grouped, dy_codes, dy_plane = [], [], [], []
        for a in range(3):
            dy_raw.append(keep.tile([P, PACK, H], F32, align_bytes=256, name="dy_raw%d" % a))
            dy_grouped.append(keep.tile([P, H, PACK], BF16, align_bytes=256, name="dy_grouped%d" % a))
            dy_codes.append(keep.tile([P, H], U32, align_bytes=256, name="dy_codes%d" % a))
            dy_plane.append(keep.tile([P, H], U8, align_bytes=256, name="dy_plane%d" % a))

        nc.vector.memset(x4_plane[:].rearrange("p a n -> p (a n)").bitcast(I32), 0)

        nc.sync.dma_start(out=x4_codes[:].bitcast(I32), in_=x4_words.rearrange("a p n -> p a n").bitcast(I32))
        nc.sync.dma_start(out=x8_raw[:], in_=x8.rearrange("(p j) d -> p j d", j=PACK))
        for q in range(4):
            nc.sync.dma_start(
                out=x4_plane[32 * q : 32 * q + 4, :, :].bitcast(I32),
                in_=x4_scales[:, 4 * q : 4 * q + 4, :].rearrange("a r n -> r a n").bitcast(I32),
            )
        for a in range(3):
            nc.sync.dma_start(out=dy_raw[a][:], in_=dy[512 * a : 512 * (a + 1), :].rearrange("(p j) h -> p j h", j=PACK))
        for m in range(0, DT, 2):
            nc.sync.dma_start(
                out=mom_sb[:, m : m + 2, :],
                in_=mom[P * m : P * (m + 2), :].rearrange("(m p) h -> p m h", p=P),
            )

        def quantize(codes, plane, grouped, fmt, w0, w1):
            nc.vector.quantize_mx(
                out=codes[:, w0:w1].bitcast(fmt),
                scales=plane[:, w0:w1],
                in_=grouped[:, w0:w1, :].rearrange("p w j -> p (w j)"),
            )

        for w0, w1 in ((0, 512), (512, 768)):
            interleave(nc.scalar.copy, x8_grouped, x8_raw, w0, w1)
        for w0, w1 in ((0, 512), (512, 768)):
            quantize(x8_codes, x8_plane, x8_grouped, E4M3, w0, w1)

        def stationary(a, m):
            cols = slice(P * m, P * (m + 1))
            if a < 2:
                return x4_codes[:, a, 2 * P * m : 2 * P * (m + 1)].bitcast(E2M1), x4_plane[:, a, cols]
            return x8_codes[:, cols].bitcast(E4M3), x8_plane[:, cols]

        acc = {}

        def multiply(a, m, h):
            if a == 0:
                bank = (HT * m + h) % BANKS
                acc[(m, h)] = psum.tile([P, NT], F32, name="acc%d" % bank)
            codes, plane = stationary(a, m)
            cols = slice(NT * h, NT * (h + 1))
            nc.tensor.matmul_mx(
                out=acc[(m, h)][:],
                lhsT=codes,
                lhsT_scale=plane,
                rhs=dy_codes[a][:, cols].bitcast(E5M2),
                rhs_scale=dy_plane[a][:, cols],
                start=(a == 0),
                stop=(a == 2),
            )

        def finish(m):
            for h in range(HT):
                cols = slice(NT * h, NT * (h + 1))
                nc.vector.scalar_tensor_tensor(
                    out=res[:, m, cols], in0=mom_sb[:, m, cols], scalar=0.9, in1=acc[(m, h)][:], op0=MULT, op1=ADD
                )
            nc.sync.dma_start(out=out[P * m : P * (m + 1), :], in_=res[:, m, :])

        early = BANKS // HT
        for a in range(3):
            interleave(nc.scalar.copy, dy_grouped[a], dy_raw[a], V_COLS, H)
            interleave(nc.vector.tensor_copy, dy_grouped[a], dy_raw[a], 0, NT)
            interleave(nc.vector.tensor_copy, dy_grouped[a], dy_raw[a], NT, V_COLS)
            for h in range(HT):
                quantize(dy_codes[a], dy_plane[a], dy_grouped[a], E5M2, NT * h, NT * (h + 1))
            for m in range(early):
                for h in range(HT):
                    multiply(a, m, h)
        for m in range(early):
            finish(m)
        for m in range(early, DT):
            for h in range(HT):
                for a in range(3):
                    multiply(a, m, h)
            finish(m)
